import numpy as np
import ml_dtypes


def mxq(x, axis, fmt="e4m3"):
    dtype, down = {"e4m3": (ml_dtypes.float8_e4m3fn, 7), "e5m2": (ml_dtypes.float8_e5m2, 14)}[fmt]
    v = np.moveaxis(np.asarray(x, np.float32).astype(ml_dtypes.bfloat16).astype(np.float64), axis, -1)
    blocks = v.reshape(v.shape[:-1] + (-1, 32))
    amax = np.abs(blocks).max(-1, keepdims=True)
    byte = np.maximum(np.where(amax > 0, np.frexp(amax)[1] - 1 + 127, 0) - down, 1)
    scale = np.exp2(byte - 127.0)
    codes = (blocks / scale).astype(np.float32).astype(dtype).astype(np.float64)
    return np.moveaxis((codes * scale).reshape(v.shape), -1, axis)


WIDE = False


def mx_kscale(k):
    if not WIDE:
        return np.ones(k)
    levels = np.array([10, -10, 5, -5, 0])
    if k % 512:
        return np.exp2(np.random.permutation(np.resize(levels, k // 32))).repeat(32)
    a = np.empty((k // 512, 16))
    for p in range(k // 512):
        a[p, :8] = np.random.permutation(np.resize(levels, 8))
        for g in range(8):
            far = levels[np.abs(levels - a[p, g]) >= 10]
            a[p, g + 8] = far[np.random.randint(len(far))]
    return np.exp2(a.ravel()).repeat(32)


BF16 = ml_dtypes.bfloat16


def bf(x):
    return np.asarray(x, np.float32).astype(BF16)


def f64(x):
    return np.asarray(x).astype(np.float64)


E2M1 = np.array([0.0, 0.5, 1.0, 1.5, 2.0, 3.0, 4.0, 6.0, -0.0, -0.5, -1.0, -1.5, -2.0, -3.0, -4.0, -6.0])


def pack_weight(w, fmt):
    k, n = w.shape
    w = f64(bf(w)).reshape(k // 32, 32, n)
    amax = np.abs(w).max(1)
    if fmt == "e4m3":
        byte = np.frexp(amax)[1] - 1 + 127 - 7
    else:
        mant, ex = np.frexp(amax / 6.0)
        byte = np.where(mant > 0.5, ex, ex - 1) + 127
    byte = np.clip(np.where(amax > 0, byte, 1), 1, 254)
    scaled = (w * np.exp2(127.0 - byte)[:, None, :]).reshape(k, n).astype(np.float32)
    by_word = np.ascontiguousarray(scaled.reshape(k // 512, 128, 4, n).transpose(0, 1, 3, 2))
    if fmt == "e4m3":
        words = by_word.astype(ml_dtypes.float8_e4m3fn).view(np.uint8)
    else:
        c = by_word.astype(ml_dtypes.float4_e2m1fn).view(np.uint8) & 0xF
        words = c[..., 0::2] | (c[..., 1::2] << 4)
    return np.ascontiguousarray(words), np.ascontiguousarray(byte.astype(np.uint8).reshape(k // 512, 16, n))


def unpack_weight(words, scales, fmt):
    g, p, n, _ = words.shape
    if fmt == "e4m3":
        vals = np.ascontiguousarray(words).view(ml_dtypes.float8_e4m3fn).astype(np.float64)
    else:
        nib = np.empty((g, p, n, 4), np.uint8)
        nib[..., 0::2] = words & 0xF
        nib[..., 1::2] = words >> 4
        vals = E2M1[nib]
    vals = vals * np.repeat(np.exp2(scales.astype(np.float64) - 127.0), 8, axis=1)[..., None]
    return vals.transpose(0, 1, 3, 2).reshape(g * 512, n)
def pack4(w):
    words, scales = pack_weight(w, "e2m1")
    return words.reshape(words.shape[0], 128, -1), scales


def unpack4(words, scales):
    return unpack_weight(words.reshape(words.shape[0], 128, -1, 2), scales, "e2m1")


def planes(Y):
    n, m = Y.shape
    b = f64(bf(Y)).reshape(n // 32, 32, m)
    amax = np.abs(b).max(1)
    byte = np.clip(np.where(amax > 0, np.frexp(amax)[1] - 1 + 127 - 7, 1), 1, 254)
    codes = (b * np.exp2(127.0 - byte)[:, None, :]).reshape(n, m).astype(np.float32).astype(ml_dtypes.float8_e4m3fn).view(np.uint8)
    words = codes.reshape(n // 512, 128, 4, m).transpose(0, 1, 3, 2)
    return np.ascontiguousarray(words), np.ascontiguousarray(byte.astype(np.uint8).reshape(n // 512, 16, m))


S, D, B = 2048, 1536, 1024
OFFSET_SIZE = 0.3
WEIGHT_SPREAD = 0.8


def setup_inputs():
    s = mx_kscale(D)
    x = np.random.randn(D, B) * s[:, None]
    x_words, x_scales = pack_weight(x, "e4m3")
    h = np.random.randn(S, D) / np.sqrt(D) / s[None, :]
    z = np.random.randn(S, B)
    offset = OFFSET_SIZE * np.random.randn(S)
    weight = np.exp(WEIGHT_SPREAD * np.random.randn(S))
    return {"x_words": x_words, "x_scales": x_scales, "h": bf(h), "z": bf(z),
            "offset": bf(offset), "weight": bf(weight)}


def reference(x_words, x_scales, h, z, offset, weight):
    x = unpack_weight(x_words, x_scales, "e4m3")
    hq = mxq(f64(h), 1, "e4m3")
    predicted = hq @ x
    innovation = f64(z) - predicted - f64(offset)[:, None]
    y = innovation * f64(weight)[:, None]
    Y = y.reshape(S, B)
    words, scales = planes(Y)
    return y, words, scales

@@ -1,0 +1,253 @@
+from contextlib import ExitStack
+
+import concourse.mybir as mybir
+from concourse.masks import make_identity
+
+S, D, B = 2048, 1536, 1024
+FLOPS = 2 * S * D * B
+
+F32 = mybir.dt.float32
+BF16 = mybir.dt.bfloat16
+U32 = mybir.dt.uint32
+I32 = mybir.dt.int32
+U8 = mybir.dt.uint8
+FP8X4 = mybir.dt.float8_e4m3fn_x4
+ALU = mybir.AluOpType
+ACT = mybir.ActivationFunctionType
+
+P = 128
+PACK = 4
+GROUP = P * PACK
+PASSES = D // GROUP
+GROUPS = S // GROUP
+TILES = GROUPS * PACK
+PAIRS = TILES // 2
+HALF = B // 2
+QUARTER = B // 4
+QUADRANTS = 4
+BANKS_PER_PAIR = 3
+WHOLE_STORES = 2
+
+
+def tile_weighted_kalman_innovation_g6_kernel(tc, x_words, x_scales, h, z, offset, weight, out_0, out_1, out_2):
+    nc = tc.nc
+    with ExitStack() as ctx:
+        keep = ctx.enter_context(tc.tile_pool(name="keep", bufs=1))
+        ring = ctx.enter_context(tc.tile_pool(name="ring", bufs=1))
+        psum = ctx.enter_context(tc.psum_pool(name="psum", bufs=4))
+        ctx.enter_context(tc.manual_schedule())
+
+        def by_slot(rows, g):
+            return rows[GROUP * g : GROUP * (g + 1), :].rearrange("(p t) m -> p t m", t=PACK)
+
+        identity = keep.tile([P, P], F32, name="identity")
+        make_identity(nc, identity[:])
+
+        x_plane = keep.tile([P, B], U8, name="x_scale_plane", align_bytes=64)
+        nc.vector.memset(x_plane[:].bitcast(U32), 0)
+
+        h_rows = {}
+        z_rows = {}
+
+        def load_h(first, count):
+            raw = keep.tile([P, count, D], BF16, name="h_raw_%d" % first)
+            g, t = divmod(first, PACK)
+            nc.sync.dma_start(out=raw[:], in_=by_slot(h, g)[:, t : t + count, :])
+            for j in range(count):
+                h_rows[first + j] = raw[:, j, :]
+
+        def load_z(g, first, width):
+            raw = keep.tile([P, PACK, width], BF16, name="z_raw_%d_%d" % (g, first))
+            nc.sync.dma_start(out=raw[:], in_=by_slot(z, g)[:, :, first : first + width])
+            for t in range(PACK):
+                for start in range(0, width, HALF):
+                    z_rows[PACK * g + t, first + start] = raw[:, t, start : start + HALF]
+
+        def load_x(half):
+            codes = keep.tile([P, PASSES, HALF], U32, name="x_codes_%d" % half, align_bytes=64)
+            source = x_words.rearrange("c p n t -> p c (n t)").bitcast(I32)
+            nc.sync.dma_start(out=codes[:].bitcast(I32), in_=source[:, :, HALF * half : HALF * (half + 1)])
+            return codes
+
+        load_h(0, 1)
+        load_h(1, 1)
+        load_h(2, 2)
+        x_codes = [load_x(0)]
+        for q in range(QUADRANTS):
+            nc.scalar.dma_start(
+                out=x_plane[32 * q : 32 * q + 4 * PASSES, :].bitcast(I32),
+                in_=x_scales[:, 4 * q : 4 * q + 4, :].bitcast(I32),
+            )
+        offset_raw = keep.tile([P, GROUPS, PACK], BF16, name="offset_raw")
+        weight_raw = keep.tile([P, GROUPS, PACK], BF16, name="weight_raw")
+        nc.gpsimd.dma_start(out=offset_raw[:], in_=offset.rearrange("(g p t) -> p g t", g=GROUPS, t=PACK))
+        nc.gpsimd.dma_start(out=weight_raw[:], in_=weight.rearrange("(g p t) -> p g t", g=GROUPS, t=PACK))
+        load_z(0, 0, HALF)
+        load_h(4, 2)
+        x_codes.append(load_x(1))
+        load_z(0, HALF, HALF)
+        for g in range(1, GROUPS):
+            load_h(PACK * g + 2, 2)
+            load_z(g, 0, B)
+            if g + 1 < GROUPS:
+                load_h(PACK * (g + 1), 2)
+
+        weights = keep.tile([P, TILES], F32, name="weights")
+        minus_weights = keep.tile([P, TILES], F32, name="minus_weights")
+        shifts = keep.tile([P, TILES], F32, name="shifts")
+
+        def sensor_constants():
+            raw = weight_raw[:].rearrange("p g t -> p (g t)")
+            nc.vector.tensor_copy(out=weights[:], in_=raw)
+            nc.vector.tensor_scalar(out=minus_weights[:], in0=raw, scalar1=-1.0, scalar2=None, op0=ALU.mult)
+            nc.vector.tensor_tensor(
+                out=shifts[:], in0=offset_raw[:].rearrange("p g t -> p (g t)"), in1=minus_weights[:], op=ALU.mult
+            )
+
+        y = [keep.tile([P, PACK, B], F32, name="y_%d" % g) for g in range(GROUPS)]
+        y_codes = [keep.tile([P, B], U32, name="y_codes_%d" % g, align_bytes=64) for g in range(GROUPS)]
+        y_plane = keep.tile([P, B], U8, name="y_scale_plane", align_bytes=64)
+
+        h_grouped = {}
+        h_codes = {}
+        y_grouped = {}
+
+        def turn_h(pair, bank):
+            turned = psum.tile([P, 2, 2, P], F32, name="turned")
+            for i in range(2):
+                slab, c = divmod(2 * (BANKS_PER_PAIR * pair + bank) + i, PASSES)
+                words = h_rows[slab].bitcast(F32)
+                for u in range(2):
+                    nc.tensor.transpose(turned[:, i, u, :], words[:, 256 * c + u : 256 * (c + 1) : 2], identity[:])
+            grouped = ring.tile([P, 2, P, PACK], BF16, name="h_grouped", bufs=4, align_bytes=64)
+            nc.scalar.copy(out=grouped[:].bitcast(F32), in_=turned[:].rearrange("p i u m -> p i m u"))
+            h_grouped[pair, bank] = grouped
+
+        def quantize_h(pair, bank):
+            codes = ring.tile([P, 2 * P], U32, name="h_codes", bufs=9, align_bytes=64)
+            plane = ring.tile([P, 2 * P], U8, name="h_scale_plane", bufs=9, align_bytes=64)
+            nc.vector.quantize_mx(
+                out=codes[:].bitcast(FP8X4),
+                scales=plane[:],
+                in_=h_grouped[pair, bank][:].rearrange("p i m t -> p (i m t)"),
+            )
+            for i in range(2):
+                columns = slice(P * i, P * (i + 1))
+                h_codes[divmod(2 * (BANKS_PER_PAIR * pair + bank) + i, PASSES)] = (codes[:, columns], plane[:, columns])
+
+        def prepare(on_scalar, slab, first):
+            g, t = divmod(slab, PACK)
+            part = y[g][:, t, first : first + HALF]
+            measured = z_rows[slab, first]
+            factor = weights[:, slab : slab + 1]
+            shift = shifts[:, slab : slab + 1]
+            if on_scalar:
+                nc.scalar.activation(out=part, in_=measured, func=ACT.Identity, bias=shift, scale=factor)
+            else:
+                nc.vector.tensor_scalar(out=part, in0=measured, scalar1=factor, scalar2=shift, op0=ALU.mult, op1=ALU.add)
+
+        def multiply(slab, first, width):
+            g, t = divmod(slab, PACK)
+            half, inside = divmod(first, HALF)
+            predicted = psum.tile([P, width], F32, name="predicted")
+            for c in range(PASSES):
+                codes, plane = h_codes[slab, c]
+                nc.tensor.matmul_mx(
+                    out=predicted[:],
+                    lhsT=codes.bitcast(FP8X4),
+                    lhsT_scale=plane,
+                    rhs=x_codes[half][:, c, inside : inside + width].bitcast(FP8X4),
+                    rhs_scale=x_plane[4 * c :, first : first + width],
+                    start=(c == 0),
+                    stop=(c == PASSES - 1),
+                )
+            part = y[g][:, t, first : first + width]
+            nc.vector.scalar_tensor_tensor(
+                out=part, in0=predicted[:], scalar=minus_weights[:, slab : slab + 1], in1=part, op0=ALU.mult, op1=ALU.add
+            )
+
+        def interleave(copy, g, first, width):
+            grouped = ring.tile([P, width, PACK], BF16, name="y_grouped", bufs=3, align_bytes=64)
+            copy(
+                out=grouped[:].rearrange("p (c i) t -> p c t i", i=4),
+                in_=y[g][:, :, first : first + width].rearrange("p t (c i) -> p c t i", i=4),
+            )
+            y_grouped[g, first] = grouped
+
+        def quantize_y(g, first, width):
+            nc.vector.quantize_mx(
+                out=y_codes[g][:, first : first + width].bitcast(FP8X4),
+                scales=y_plane[4 * g :, first : first + width],
+                in_=y_grouped[g, first][:].rearrange("p m t -> p (m t)"),
+            )
+
+        def store_y(g, slots, first, width):
+            nc.sync.dma_start(out=by_slot(out_0, g)[:, slots, first : first + width], in_=y[g][:, slots, first : first + width])
+
+        def store_codes(g, first, width):
+            target = out_1[g].rearrange("p m t -> p (m t)").bitcast(I32)
+            nc.sync.dma_start(out=target[:, first : first + width], in_=y_codes[g][:, first : first + width].bitcast(I32))
+
+        def store_scales(first, width):
+            for q in range(QUADRANTS):
+                nc.scalar.dma_start(
+                    out=out_2[:, 4 * q : 4 * q + 4, first : first + width].bitcast(I32),
+                    in_=y_plane[32 * q : 32 * q + 4 * GROUPS, first : first + width].bitcast(I32),
+                )
+
+        last = GROUPS - 1
+        every = slice(0, PACK)
+
+        for bank in range(BANKS_PER_PAIR):
+            turn_h(0, bank)
+            quantize_h(0, bank)
+        sensor_constants()
+
+        for step in range(2 * GROUPS - 1):
+            g, half = divmod(step, 2)
+            next_g, next_half = divmod(step + 1, 2)
+            for bank in range(BANKS_PER_PAIR):
+                turn_h(step + 1, bank)
+            if step >= 2:
+                done_g, done_half = divmod(step - 2, 2)
+                quantize_y(done_g, HALF * done_half, HALF)
+                if done_half:
+                    store_codes(done_g, 0, B)
+            if step == 1:
+                prepare(True, PACK - 1, HALF)
+            if step >= 1:
+                interleave(nc.scalar.copy, (step - 1) // 2, HALF * (1 - half), HALF)
+            for bank in range(BANKS_PER_PAIR):
+                quantize_h(step + 1, bank)
+            if step == 0:
+                for t in range(PACK):
+                    prepare(t >= 2, t, 0)
+            if step == 1:
+                for t in range(PACK - 1):
+                    prepare(False, t, HALF)
+            for t in range(PACK):
+                multiply(PACK * g + t, HALF * half, HALF)
+                if step >= 1:
+                    prepare(t == PACK - 1, PACK * next_g + t, HALF * next_half)
+            if g >= WHOLE_STORES:
+                store_y(g, every, HALF * half, HALF)
+            elif half:
+                store_y(g, every, 0, B)
+
+        interleave(nc.scalar.copy, last, 0, HALF)
+        quantize_y(last - 1, HALF, HALF)
+        store_codes(last - 1, 0, B)
+        for t in range(PACK):
+            multiply(PACK * last + t, HALF, QUARTER)
+        store_y(last, every, HALF, QUARTER)
+        interleave(nc.scalar.copy, last, HALF, QUARTER)
+        for t in range(PACK):
+            multiply(PACK * last + t, HALF + QUARTER, QUARTER)
+        store_y(last, every, HALF + QUARTER, QUARTER)
+        quantize_y(last, 0, HALF)
+        interleave(nc.vector.tensor_copy, last, HALF + QUARTER, QUARTER)
+        quantize_y(last, HALF, QUARTER)
+        store_codes(last, 0, HALF + QUARTER)
+        quantize_y(last, HALF + QUARTER, QUARTER)
+        store_codes(last, HALF + QUARTER, QUARTER)
+        store_scales(0, B)

@@ -27,6 +27,8 @@ QUARTER = B // 4
 QUADRANTS = 4
 BANKS_PER_PAIR = 3
 WHOLE_STORES = 2
+TURN_BANKS = 3
+SUM_BANKS = 5
 
 
 def tile_weighted_kalman_innovation_g6_kernel(tc, x_words, x_scales, h, z, offset, weight, out_0, out_1, out_2):
@@ -34,7 +36,7 @@ def tile_weighted_kalman_innovation_g6_kernel(tc, x_words, x_scales, h, z, offse
     with ExitStack() as ctx:
         keep = ctx.enter_context(tc.tile_pool(name="keep", bufs=1))
         ring = ctx.enter_context(tc.tile_pool(name="ring", bufs=1))
-        psum = ctx.enter_context(tc.psum_pool(name="psum", bufs=4))
+        psum = ctx.enter_context(tc.psum_pool(name="psum", bufs=1))
         ctx.enter_context(tc.manual_schedule())
 
         def by_slot(rows, g):
@@ -42,6 +44,9 @@ def tile_weighted_kalman_innovation_g6_kernel(tc, x_words, x_scales, h, z, offse
 
         identity = keep.tile([P, P], F32, name="identity")
         make_identity(nc, identity[:])
+
+        sensor_rows = keep.tile([P, GROUP], BF16, name="sensor_rows")
+        nc.vector.memset(sensor_rows[:].bitcast(F32), 0.0)
 
         x_plane = keep.tile([P, B], U8, name="x_scale_plane", align_bytes=64)
         nc.vector.memset(x_plane[:].bitcast(U32), 0)
@@ -71,6 +76,8 @@ def tile_weighted_kalman_innovation_g6_kernel(tc, x_words, x_scales, h, z, offse
 
         load_h(0, 1)
         load_h(1, 1)
+        nc.sync.dma_start(out=sensor_rows[0:GROUPS, :], in_=weight.rearrange("(g s) -> g s", g=GROUPS))
+        nc.sync.dma_start(out=sensor_rows[GROUPS : 2 * GROUPS, :], in_=offset.rearrange("(g s) -> g s", g=GROUPS))
         load_h(2, 2)
         x_codes = [load_x(0)]
         for q in range(QUADRANTS):
@@ -78,10 +85,6 @@ def tile_weighted_kalman_innovation_g6_kernel(tc, x_words, x_scales, h, z, offse
                 out=x_plane[32 * q : 32 * q + 4 * PASSES, :].bitcast(I32),
                 in_=x_scales[:, 4 * q : 4 * q + 4, :].bitcast(I32),
             )
-        offset_raw = keep.tile([P, GROUPS, PACK], BF16, name="offset_raw")
-        weight_raw = keep.tile([P, GROUPS, PACK], BF16, name="weight_raw")
-        nc.gpsimd.dma_start(out=offset_raw[:], in_=offset.rearrange("(g p t) -> p g t", g=GROUPS, t=PACK))
-        nc.gpsimd.dma_start(out=weight_raw[:], in_=weight.rearrange("(g p t) -> p g t", g=GROUPS, t=PACK))
         load_z(0, 0, HALF)
         load_h(4, 2)
         x_codes.append(load_x(1))
@@ -97,11 +100,22 @@ def tile_weighted_kalman_innovation_g6_kernel(tc, x_words, x_scales, h, z, offse
         shifts = keep.tile([P, TILES], F32, name="shifts")
 
         def sensor_constants():
-            raw = weight_raw[:].rearrange("p g t -> p (g t)")
-            nc.vector.tensor_copy(out=weights[:], in_=raw)
-            nc.vector.tensor_scalar(out=minus_weights[:], in0=raw, scalar1=-1.0, scalar2=None, op0=ALU.mult)
+            turned = psum.tile([P, 2, P], F32, name="predicted", bufs=SUM_BANKS)
+            words = sensor_rows[:].bitcast(F32)
+            for u in range(2):
+                nc.tensor.transpose(turned[:, u, :], words[:, u : 2 * P : 2], identity[:])
+            values = turned[:, :, 0 : 2 * GROUPS].bitcast(BF16).rearrange("p u (r e) -> p r u e", e=2)
+            by_slab = "p (g u e) -> p g u e"
+            raw_weights = values[:, 0:GROUPS, :, :]
+            nc.vector.tensor_copy(out=weights[:].rearrange(by_slab, u=2, e=2), in_=raw_weights)
+            nc.vector.tensor_scalar(
+                out=minus_weights[:].rearrange(by_slab, u=2, e=2), in0=raw_weights, scalar1=-1.0, scalar2=None, op0=ALU.mult
+            )
             nc.vector.tensor_tensor(
-                out=shifts[:], in0=offset_raw[:].rearrange("p g t -> p (g t)"), in1=minus_weights[:], op=ALU.mult
+                out=shifts[:].rearrange(by_slab, u=2, e=2),
+                in0=values[:, GROUPS : 2 * GROUPS, :, :],
+                in1=minus_weights[:].rearrange(by_slab, u=2, e=2),
+                op=ALU.mult,
             )
 
         y = [keep.tile([P, PACK, B], F32, name="y_%d" % g) for g in range(GROUPS)]
@@ -113,7 +127,7 @@ def tile_weighted_kalman_innovation_g6_kernel(tc, x_words, x_scales, h, z, offse
         y_grouped = {}
 
         def turn_h(pair, bank):
-            turned = psum.tile([P, 2, 2, P], F32, name="turned")
+            turned = psum.tile([P, 2, 2, P], F32, name="turned", bufs=TURN_BANKS)
             for i in range(2):
                 slab, c = divmod(2 * (BANKS_PER_PAIR * pair + bank) + i, PASSES)
                 words = h_rows[slab].bitcast(F32)
@@ -149,7 +163,7 @@ def tile_weighted_kalman_innovation_g6_kernel(tc, x_words, x_scales, h, z, offse
         def multiply(slab, first, width):
             g, t = divmod(slab, PACK)
             half, inside = divmod(first, HALF)
-            predicted = psum.tile([P, width], F32, name="predicted")
+            predicted = psum.tile([P, width], F32, name="predicted", bufs=SUM_BANKS)
             for c in range(PASSES):
                 codes, plane = h_codes[slab, c]
                 nc.tensor.matmul_mx(
@@ -229,9 +243,9 @@ def tile_weighted_kalman_innovation_g6_kernel(tc, x_words, x_scales, h, z, offse
                 multiply(PACK * g + t, HALF * half, HALF)
                 if step >= 1:
                     prepare(t == PACK - 1, PACK * next_g + t, HALF * next_half)
-            if g >= WHOLE_STORES:
-                store_y(g, every, HALF * half, HALF)
-            elif half:
+                if g >= WHOLE_STORES and t % 2:
+                    store_y(g, slice(t - 1, t + 1), HALF * half, HALF)
+            if g < WHOLE_STORES and half:
                 store_y(g, every, 0, B)
 
         interleave(nc.scalar.copy, last, 0, HALF)

@@ -61,12 +61,11 @@ def tile_weighted_kalman_innovation_g6_kernel(tc, x_words, x_scales, h, z, offse
             for j in range(count):
                 h_rows[first + j] = raw[:, j, :]
 
-        def load_z(g, first, width):
-            raw = keep.tile([P, PACK, width], BF16, name="z_raw_%d_%d" % (g, first))
-            nc.sync.dma_start(out=raw[:], in_=by_slot(z, g)[:, :, first : first + width])
+        def load_z(g):
+            raw = keep.tile([P, PACK, B], BF16, name="z_raw_%d" % g)
+            nc.sync.dma_start(out=raw[:], in_=by_slot(z, g))
             for t in range(PACK):
-                for start in range(0, width, HALF):
-                    z_rows[PACK * g + t, first + start] = raw[:, t, start : start + HALF]
+                z_rows[PACK * g + t] = raw[:, t, :]
 
         def load_x(half):
             codes = keep.tile([P, PASSES, HALF], U32, name="x_codes_%d" % half, align_bytes=64)
@@ -81,17 +80,16 @@ def tile_weighted_kalman_innovation_g6_kernel(tc, x_words, x_scales, h, z, offse
         load_h(2, 2)
         x_codes = [load_x(0)]
         for q in range(QUADRANTS):
-            nc.scalar.dma_start(
+            nc.sync.dma_start(
                 out=x_plane[32 * q : 32 * q + 4 * PASSES, :].bitcast(I32),
                 in_=x_scales[:, 4 * q : 4 * q + 4, :].bitcast(I32),
             )
-        load_z(0, 0, HALF)
+        load_z(0)
         load_h(4, 2)
         x_codes.append(load_x(1))
-        load_z(0, HALF, HALF)
         for g in range(1, GROUPS):
             load_h(PACK * g + 2, 2)
-            load_z(g, 0, B)
+            load_z(g)
             if g + 1 < GROUPS:
                 load_h(PACK * (g + 1), 2)
 
@@ -125,6 +123,8 @@ def tile_weighted_kalman_innovation_g6_kernel(tc, x_words, x_scales, h, z, offse
         h_grouped = {}
         h_codes = {}
         y_grouped = {}
+        prepared = {}
+        blocks = [(PACK * g + t, first) for g in range(GROUPS) for first in (0, HALF) for t in range(PACK)]
 
         def turn_h(pair, bank):
             turned = psum.tile([P, 2, 2, P], F32, name="turned", bufs=TURN_BANKS)
@@ -149,16 +149,20 @@ def tile_weighted_kalman_innovation_g6_kernel(tc, x_words, x_scales, h, z, offse
                 columns = slice(P * i, P * (i + 1))
                 h_codes[divmod(2 * (BANKS_PER_PAIR * pair + bank) + i, PASSES)] = (codes[:, columns], plane[:, columns])
 
-        def prepare(on_scalar, slab, first):
-            g, t = divmod(slab, PACK)
-            part = y[g][:, t, first : first + HALF]
-            measured = z_rows[slab, first]
+        def prepare(engine, n):
+            slab, first = blocks[n]
+            if n % PACK == PACK - 1:
+                part = ring.tile([P, HALF], F32, name="prepared_last", bufs=2)
+            else:
+                part = ring.tile([P, HALF], F32, name="prepared", bufs=PACK - 1)
+            measured = z_rows[slab][:, first : first + HALF]
             factor = weights[:, slab : slab + 1]
             shift = shifts[:, slab : slab + 1]
-            if on_scalar:
-                nc.scalar.activation(out=part, in_=measured, func=ACT.Identity, bias=shift, scale=factor)
+            if engine is nc.scalar:
+                nc.scalar.activation(out=part[:], in_=measured, func=ACT.Identity, bias=shift, scale=factor)
             else:
-                nc.vector.tensor_scalar(out=part, in0=measured, scalar1=factor, scalar2=shift, op0=ALU.mult, op1=ALU.add)
+                engine.tensor_scalar(out=part[:], in0=measured, scalar1=factor, scalar2=shift, op0=ALU.mult, op1=ALU.add)
+            prepared[slab, first] = part
 
         def multiply(slab, first, width):
             g, t = divmod(slab, PACK)
@@ -175,9 +179,13 @@ def tile_weighted_kalman_innovation_g6_kernel(tc, x_words, x_scales, h, z, offse
                     start=(c == 0),
                     stop=(c == PASSES - 1),
                 )
-            part = y[g][:, t, first : first + width]
             nc.vector.scalar_tensor_tensor(
-                out=part, in0=predicted[:], scalar=minus_weights[:, slab : slab + 1], in1=part, op0=ALU.mult, op1=ALU.add
+                out=y[g][:, t, first : first + width],
+                in0=predicted[:],
+                scalar=minus_weights[:, slab : slab + 1],
+                in1=prepared[slab, HALF * half][:, inside : inside + width],
+                op0=ALU.mult,
+                op1=ALU.add,
             )
 
         def interleave(copy, g, first, width):
@@ -209,48 +217,55 @@ def tile_weighted_kalman_innovation_g6_kernel(tc, x_words, x_scales, h, z, offse
                     in_=y_plane[32 * q : 32 * q + 4 * GROUPS, first : first + width].bitcast(I32),
                 )
 
+        def turn_pair(pair):
+            for bank in range(BANKS_PER_PAIR):
+                turn_h(pair, bank)
+
+        def quantize_pair(pair):
+            for bank in range(BANKS_PER_PAIR):
+                quantize_h(pair, bank)
+
+        def block(n):
+            multiply(*blocks[n], HALF)
+            if n % PACK != PACK - 1:
+                prepare(nc.gpsimd, n + PACK)
+
         last = GROUPS - 1
         every = slice(0, PACK)
 
-        for bank in range(BANKS_PER_PAIR):
-            turn_h(0, bank)
-            quantize_h(0, bank)
+        turn_pair(0)
+        quantize_pair(0)
         sensor_constants()
 
         for step in range(2 * GROUPS - 1):
             g, half = divmod(step, 2)
-            next_g, next_half = divmod(step + 1, 2)
-            for bank in range(BANKS_PER_PAIR):
-                turn_h(step + 1, bank)
+            turn_pair(step + 1)
+            if step >= 1:
+                interleave(nc.scalar.copy, (step - 1) // 2, HALF * (1 - half), HALF)
             if step >= 2:
                 done_g, done_half = divmod(step - 2, 2)
                 quantize_y(done_g, HALF * done_half, HALF)
                 if done_half:
                     store_codes(done_g, 0, B)
-            if step == 1:
-                prepare(True, PACK - 1, HALF)
             if step >= 1:
-                interleave(nc.scalar.copy, (step - 1) // 2, HALF * (1 - half), HALF)
-            for bank in range(BANKS_PER_PAIR):
-                quantize_h(step + 1, bank)
+                prepare(nc.vector, PACK * step + PACK - 1)
+            quantize_pair(step + 1)
             if step == 0:
-                for t in range(PACK):
-                    prepare(t >= 2, t, 0)
-            if step == 1:
-                for t in range(PACK - 1):
-                    prepare(False, t, HALF)
+                for n in range(PACK):
+                    prepare(nc.scalar if n >= 2 else nc.vector, n)
+            if g == last:
+                prepare(nc.scalar, len(blocks) - 1)
             for t in range(PACK):
-                multiply(PACK * g + t, HALF * half, HALF)
-                if step >= 1:
-                    prepare(t == PACK - 1, PACK * next_g + t, HALF * next_half)
+                block(PACK * step + t)
+                if g == last and t == PACK - 2:
+                    quantize_y(last - 1, HALF, HALF)
+                    store_codes(last - 1, 0, B)
                 if g >= WHOLE_STORES and t % 2:
                     store_y(g, slice(t - 1, t + 1), HALF * half, HALF)
             if g < WHOLE_STORES and half:
                 store_y(g, every, 0, B)
 
         interleave(nc.scalar.copy, last, 0, HALF)
-        quantize_y(last - 1, HALF, HALF)
-        store_codes(last - 1, 0, B)
         for t in range(PACK):
             multiply(PACK * last + t, HALF, QUARTER)
         store_y(last, every, HALF, QUARTER)

from contextlib import ExitStack

import concourse.mybir as mybir
from concourse.masks import make_identity

S, D, B = 2048, 1536, 1024
FLOPS = 2 * S * D * B

F32 = mybir.dt.float32
BF16 = mybir.dt.bfloat16
U32 = mybir.dt.uint32
I32 = mybir.dt.int32
U8 = mybir.dt.uint8
FP8X4 = mybir.dt.float8_e4m3fn_x4
ALU = mybir.AluOpType
ACT = mybir.ActivationFunctionType

P = 128
PACK = 4
GROUP = P * PACK
PASSES = D // GROUP
GROUPS = S // GROUP
TILES = GROUPS * PACK
PAIRS = TILES // 2
HALF = B // 2
QUARTER = B // 4
QUADRANTS = 4
BANKS_PER_PAIR = 3
WHOLE_STORES = 2
TURN_BANKS = 3
SUM_BANKS = 5


def tile_weighted_kalman_innovation_g6_kernel(tc, x_words, x_scales, h, z, offset, weight, out_0, out_1, out_2):
    nc = tc.nc
    with ExitStack() as ctx:
        keep = ctx.enter_context(tc.tile_pool(name="keep", bufs=1))
        ring = ctx.enter_context(tc.tile_pool(name="ring", bufs=1))
        psum = ctx.enter_context(tc.psum_pool(name="psum", bufs=1))
        ctx.enter_context(tc.manual_schedule())

        def by_slot(rows, g):
            return rows[GROUP * g : GROUP * (g + 1), :].rearrange("(p t) m -> p t m", t=PACK)

        identity = keep.tile([P, P], F32, name="identity")
        make_identity(nc, identity[:])

        sensor_rows = keep.tile([P, GROUP], BF16, name="sensor_rows")
        nc.vector.memset(sensor_rows[:].bitcast(F32), 0.0)

        x_plane = keep.tile([P, B], U8, name="x_scale_plane", align_bytes=64)
        nc.vector.memset(x_plane[:].bitcast(U32), 0)

        h_rows = {}
        z_rows = {}

        def load_h(first, count):
            raw = keep.tile([P, count, D], BF16, name="h_raw_%d" % first)
            g, t = divmod(first, PACK)
            nc.sync.dma_start(out=raw[:], in_=by_slot(h, g)[:, t : t + count, :])
            for j in range(count):
                h_rows[first + j] = raw[:, j, :]

        def load_z(g):
            raw = keep.tile([P, PACK, B], BF16, name="z_raw_%d" % g)
            nc.sync.dma_start(out=raw[:], in_=by_slot(z, g))
            for t in range(PACK):
                z_rows[PACK * g + t] = raw[:, t, :]

        def load_x(half):
            codes = keep.tile([P, PASSES, HALF], U32, name="x_codes_%d" % half, align_bytes=64)
            source = x_words.rearrange("c p n t -> p c (n t)").bitcast(I32)
            nc.sync.dma_start(out=codes[:].bitcast(I32), in_=source[:, :, HALF * half : HALF * (half + 1)])
            return codes

        load_h(0, 1)
        load_h(1, 1)
        nc.sync.dma_start(out=sensor_rows[0:GROUPS, :], in_=weight.rearrange("(g s) -> g s", g=GROUPS))
        nc.sync.dma_start(out=sensor_rows[GROUPS : 2 * GROUPS, :], in_=offset.rearrange("(g s) -> g s", g=GROUPS))
        load_h(2, 2)
        x_codes = [load_x(0)]
        for q in range(QUADRANTS):
            nc.sync.dma_start(
                out=x_plane[32 * q : 32 * q + 4 * PASSES, :].bitcast(I32),
                in_=x_scales[:, 4 * q : 4 * q + 4, :].bitcast(I32),
            )
        load_z(0)
        load_h(4, 2)
        x_codes.append(load_x(1))
        for g in range(1, GROUPS):
            load_h(PACK * g + 2, 2)
            load_z(g)
            if g + 1 < GROUPS:
                load_h(PACK * (g + 1), 2)

        weights = keep.tile([P, TILES], F32, name="weights")
        minus_weights = keep.tile([P, TILES], F32, name="minus_weights")
        shifts = keep.tile([P, TILES], F32, name="shifts")

        def sensor_constants():
            turned = psum.tile([P, 2, P], F32, name="predicted", bufs=SUM_BANKS)
            words = sensor_rows[:].bitcast(F32)
            for u in range(2):
                nc.tensor.transpose(turned[:, u, :], words[:, u : 2 * P : 2], identity[:])
            values = turned[:, :, 0 : 2 * GROUPS].bitcast(BF16).rearrange("p u (r e) -> p r u e", e=2)
            by_slab = "p (g u e) -> p g u e"
            raw_weights = values[:, 0:GROUPS, :, :]
            nc.vector.tensor_copy(out=weights[:].rearrange(by_slab, u=2, e=2), in_=raw_weights)
            nc.vector.tensor_scalar(
                out=minus_weights[:].rearrange(by_slab, u=2, e=2), in0=raw_weights, scalar1=-1.0, scalar2=None, op0=ALU.mult
            )
            nc.vector.tensor_tensor(
                out=shifts[:].rearrange(by_slab, u=2, e=2),
                in0=values[:, GROUPS : 2 * GROUPS, :, :],
                in1=minus_weights[:].rearrange(by_slab, u=2, e=2),
                op=ALU.mult,
            )

        y = [keep.tile([P, PACK, B], F32, name="y_%d" % g) for g in range(GROUPS)]
        y_codes = [keep.tile([P, B], U32, name="y_codes_%d" % g, align_bytes=64) for g in range(GROUPS)]
        y_plane = keep.tile([P, B], U8, name="y_scale_plane", align_bytes=64)

        h_grouped = {}
        h_codes = {}
        y_grouped = {}
        prepared = {}
        blocks = [(PACK * g + t, first) for g in range(GROUPS) for first in (0, HALF) for t in range(PACK)]

        def turn_h(pair, bank):
            turned = psum.tile([P, 2, 2, P], F32, name="turned", bufs=TURN_BANKS)
            for i in range(2):
                slab, c = divmod(2 * (BANKS_PER_PAIR * pair + bank) + i, PASSES)
                words = h_rows[slab].bitcast(F32)
                for u in range(2):
                    nc.tensor.transpose(turned[:, i, u, :], words[:, 256 * c + u : 256 * (c + 1) : 2], identity[:])
            grouped = ring.tile([P, 2, P, PACK], BF16, name="h_grouped", bufs=4, align_bytes=64)
            nc.scalar.copy(out=grouped[:].bitcast(F32), in_=turned[:].rearrange("p i u m -> p i m u"))
            h_grouped[pair, bank] = grouped

        def quantize_h(pair, bank):
            codes = ring.tile([P, 2 * P], U32, name="h_codes", bufs=9, align_bytes=64)
            plane = ring.tile([P, 2 * P], U8, name="h_scale_plane", bufs=9, align_bytes=64)
            nc.vector.quantize_mx(
                out=codes[:].bitcast(FP8X4),
                scales=plane[:],
                in_=h_grouped[pair, bank][:].rearrange("p i m t -> p (i m t)"),
            )
            for i in range(2):
                columns = slice(P * i, P * (i + 1))
                h_codes[divmod(2 * (BANKS_PER_PAIR * pair + bank) + i, PASSES)] = (codes[:, columns], plane[:, columns])

        def prepare(engine, n):
            slab, first = blocks[n]
            if n % PACK == PACK - 1:
                part = ring.tile([P, HALF], F32, name="prepared_last", bufs=2)
            else:
                part = ring.tile([P, HALF], F32, name="prepared", bufs=PACK - 1)
            measured = z_rows[slab][:, first : first + HALF]
            factor = weights[:, slab : slab + 1]
            shift = shifts[:, slab : slab + 1]
            if engine is nc.scalar:
                nc.scalar.activation(out=part[:], in_=measured, func=ACT.Identity, bias=shift, scale=factor)
            else:
                engine.tensor_scalar(out=part[:], in0=measured, scalar1=factor, scalar2=shift, op0=ALU.mult, op1=ALU.add)
            prepared[slab, first] = part

        def multiply(slab, first, width):
            g, t = divmod(slab, PACK)
            half, inside = divmod(first, HALF)
            predicted = psum.tile([P, width], F32, name="predicted", bufs=SUM_BANKS)
            for c in range(PASSES):
                codes, plane = h_codes[slab, c]
                nc.tensor.matmul_mx(
                    out=predicted[:],
                    lhsT=codes.bitcast(FP8X4),
                    lhsT_scale=plane,
                    rhs=x_codes[half][:, c, inside : inside + width].bitcast(FP8X4),
                    rhs_scale=x_plane[4 * c :, first : first + width],
                    start=(c == 0),
                    stop=(c == PASSES - 1),
                )
            nc.vector.scalar_tensor_tensor(
                out=y[g][:, t, first : first + width],
                in0=predicted[:],
                scalar=minus_weights[:, slab : slab + 1],
                in1=prepared[slab, HALF * half][:, inside : inside + width],
                op0=ALU.mult,
                op1=ALU.add,
            )

        def interleave(copy, g, first, width):
            grouped = ring.tile([P, width, PACK], BF16, name="y_grouped", bufs=3, align_bytes=64)
            copy(
                out=grouped[:].rearrange("p (c i) t -> p c t i", i=4),
                in_=y[g][:, :, first : first + width].rearrange("p t (c i) -> p c t i", i=4),
            )
            y_grouped[g, first] = grouped

        def quantize_y(g, first, width):
            nc.vector.quantize_mx(
                out=y_codes[g][:, first : first + width].bitcast(FP8X4),
                scales=y_plane[4 * g :, first : first + width],
                in_=y_grouped[g, first][:].rearrange("p m t -> p (m t)"),
            )

        def store_y(g, slots, first, width):
            nc.sync.dma_start(out=by_slot(out_0, g)[:, slots, first : first + width], in_=y[g][:, slots, first : first + width])

        def store_codes(g, first, width):
            target = out_1[g].rearrange("p m t -> p (m t)").bitcast(I32)
            nc.sync.dma_start(out=target[:, first : first + width], in_=y_codes[g][:, first : first + width].bitcast(I32))

        def store_scales(first, width):
            for q in range(QUADRANTS):
                nc.scalar.dma_start(
                    out=out_2[:, 4 * q : 4 * q + 4, first : first + width].bitcast(I32),
                    in_=y_plane[32 * q : 32 * q + 4 * GROUPS, first : first + width].bitcast(I32),
                )

        def turn_pair(pair):
            for bank in range(BANKS_PER_PAIR):
                turn_h(pair, bank)

        def quantize_pair(pair):
            for bank in range(BANKS_PER_PAIR):
                quantize_h(pair, bank)

        def block(n):
            multiply(*blocks[n], HALF)
            if n % PACK != PACK - 1:
                prepare(nc.gpsimd, n + PACK)

        last = GROUPS - 1
        every = slice(0, PACK)

        turn_pair(0)
        quantize_pair(0)
        sensor_constants()

        for step in range(2 * GROUPS - 1):
            g, half = divmod(step, 2)
            turn_pair(step + 1)
            if step >= 1:
                interleave(nc.scalar.copy, (step - 1) // 2, HALF * (1 - half), HALF)
            if step >= 2:
                done_g, done_half = divmod(step - 2, 2)
                quantize_y(done_g, HALF * done_half, HALF)
                if done_half:
                    store_codes(done_g, 0, B)
            if step >= 1:
                prepare(nc.vector, PACK * step + PACK - 1)
            quantize_pair(step + 1)
            if step == 0:
                for n in range(PACK):
                    prepare(nc.scalar if n >= 2 else nc.vector, n)
            if g == last:
                prepare(nc.scalar, len(blocks) - 1)
            for t in range(PACK):
                block(PACK * step + t)
                if g == last and t == PACK - 2:
                    quantize_y(last - 1, HALF, HALF)
                    store_codes(last - 1, 0, B)
                if g >= WHOLE_STORES and t % 2:
                    store_y(g, slice(t - 1, t + 1), HALF * half, HALF)
            if g < WHOLE_STORES and half:
                store_y(g, every, 0, B)

        interleave(nc.scalar.copy, last, 0, HALF)
        for t in range(PACK):
            multiply(PACK * last + t, HALF, QUARTER)
        store_y(last, every, HALF, QUARTER)
        interleave(nc.scalar.copy, last, HALF, QUARTER)
        for t in range(PACK):
            multiply(PACK * last + t, HALF + QUARTER, QUARTER)
        store_y(last, every, HALF + QUARTER, QUARTER)
        quantize_y(last, 0, HALF)
        interleave(nc.vector.tensor_copy, last, HALF + QUARTER, QUARTER)
        quantize_y(last, HALF, QUARTER)
        store_codes(last, 0, HALF + QUARTER)
        quantize_y(last, HALF + QUARTER, QUARTER)
        store_codes(last, HALF + QUARTER, QUARTER)
        store_scales(0, B)
